import numpy as np
import ml_dtypes


def mxq(x, axis, fmt="e4m3"):
    dtype, down = {"e4m3": (ml_dtypes.float8_e4m3fn, 7), "e5m2": (ml_dtypes.float8_e5m2, 14)}[fmt]
    v = np.moveaxis(np.asarray(x, np.float32).astype(ml_dtypes.bfloat16).astype(np.float64), axis, -1)
    blocks = v.reshape(v.shape[:-1] + (-1, 32))
    amax = np.abs(blocks).max(-1, keepdims=True)
    byte = np.maximum(np.where(amax > 0, np.frexp(amax)[1] - 1 + 127, 0) - down, 1)
    scale = np.exp2(byte - 127.0)
    codes = (blocks / scale).astype(np.float32).astype(dtype).astype(np.float64)
    return np.moveaxis((codes * scale).reshape(v.shape), -1, axis)


WIDE = False


def mx_kscale(k):
    if not WIDE:
        return np.ones(k)
    levels = np.array([10, -10, 5, -5, 0])
    if k % 512:
        return np.exp2(np.random.permutation(np.resize(levels, k // 32))).repeat(32)
    a = np.empty((k // 512, 16))
    for p in range(k // 512):
        a[p, :8] = np.random.permutation(np.resize(levels, 8))
        for g in range(8):
            far = levels[np.abs(levels - a[p, g]) >= 10]
            a[p, g + 8] = far[np.random.randint(len(far))]
    return np.exp2(a.ravel()).repeat(32)


def f64(x):
    return np.asarray(x).astype(np.float64)


def striped(idx):
    return np.tile(idx.reshape(-1, 16).T, (8, 1)).astype(np.uint16)


def unstriped(offs):
    return offs[:16].T.reshape(-1).astype(np.int64)


E2M1 = np.array([0.0, 0.5, 1.0, 1.5, 2.0, 3.0, 4.0, 6.0, -0.0, -0.5, -1.0, -1.5, -2.0, -3.0, -4.0, -6.0])


def pack_weight(w, fmt):
    k, n = w.shape
    w = f64(np.asarray(w, np.float32).astype(ml_dtypes.bfloat16)).reshape(k // 32, 32, n)
    amax = np.abs(w).max(1)
    if fmt == "e4m3":
        byte = np.frexp(amax)[1] - 1 + 127 - 7
    else:
        mant, ex = np.frexp(amax / 6.0)
        byte = np.where(mant > 0.5, ex, ex - 1) + 127
    byte = np.clip(np.where(amax > 0, byte, 1), 1, 254)
    scaled = (w * np.exp2(127.0 - byte)[:, None, :]).reshape(k, n).astype(np.float32)
    by_word = np.ascontiguousarray(scaled.reshape(k // 512, 128, 4, n).transpose(0, 1, 3, 2))
    if fmt == "e4m3":
        words = by_word.astype(ml_dtypes.float8_e4m3fn).view(np.uint8)
    else:
        c = by_word.astype(ml_dtypes.float4_e2m1fn).view(np.uint8) & 0xF
        words = (c[..., 0::2] | (c[..., 1::2] << 4)).reshape(k // 512, 128, 2 * n)
    return np.ascontiguousarray(words), np.ascontiguousarray(byte.astype(np.uint8).reshape(k // 512, 16, n))


def unpack_weight(words, scales, fmt):
    g, _, n = scales.shape
    words = np.ascontiguousarray(words).reshape(g, 128, n, -1)
    if fmt == "e4m3":
        vals = words.view(ml_dtypes.float8_e4m3fn).astype(np.float64)
    else:
        nib = np.empty((g, 128, n, 4), np.uint8)
        nib[..., 0::2] = words & 0xF
        nib[..., 1::2] = words >> 4
        vals = E2M1[nib]
    vals = vals * np.repeat(np.exp2(scales.astype(np.float64) - 127.0), 8, axis=1)[..., None]
    return vals.transpose(0, 1, 3, 2).reshape(g * 512, n)


def gelu(v):
    return 0.5 * v * (1.0 + np.tanh(np.sqrt(2.0 / np.pi) * (v + 0.044715 * v**3)))


def bf(x):
    return np.asarray(x, np.float32).astype(ml_dtypes.bfloat16)


def planes(Y):
    n, m = Y.shape
    b = f64(bf(Y)).reshape(n // 32, 32, m)
    amax = np.abs(b).max(1)
    byte = np.clip(np.where(amax > 0, np.frexp(amax)[1] - 1 + 127 - 7, 1), 1, 254)
    codes = (b * np.exp2(127.0 - byte)[:, None, :]).reshape(n, m).astype(np.float32).astype(ml_dtypes.float8_e4m3fn).view(np.uint8)
    words = codes.reshape(n // 512, 128, 4, m).transpose(0, 1, 3, 2)
    return np.ascontiguousarray(words), np.ascontiguousarray(byte.astype(np.uint8).reshape(n // 512, 16, m))


K, H, N, S, T, K2, P, TV = 1024, 512, 1024, 1024, 4096, 512, 512, 2048

def setup_inputs():
    n = np.random.standard_normal
    s = mx_kscale(K)[:, None]
    s2 = mx_kscale(K2)[:, None]
    u = mx_kscale(H)[:, None]
    size = np.exp(0.8 * n(N) + np.linspace(-2.0, 1.0, N))
    tab_words, tab_scales = pack_weight(n((K, T)) * s, "e4m3")
    tab2_words, tab2_scales = pack_weight(n((K2, TV)) * s2, "e4m3")
    w2_words, w2_scales = pack_weight(1.3 * n((K, H)) / (s * np.sqrt(K)), "e2m1")
    w4_words, w4_scales = pack_weight(0.9 * n((K2, N)) / (s2 * np.sqrt(K2)), "e4m3")
    return {
        "tab_words": tab_words, "tab_scales": tab_scales,
        "offs": striped(np.random.permutation(T)[:S]),
        "tab2_words": tab2_words, "tab2_scales": tab2_scales,
        "offs2": striped(np.random.permutation(TV)[:P]),
        "pos1": striped(np.random.permutation(S)[:P]),
        "w1": (0.57 * n((K, H)) / (s * np.sqrt(K))).astype(np.float32),
        "w2_words": w2_words, "w2_scales": w2_scales,
        "amp": (u[:, 0] * np.exp(0.3 * n(H))).astype(np.float32),
        "w5": (0.33 * n((H, N)) * size / (u * np.sqrt(H))).astype(np.float32),
        "w3": (0.3 * n((K2, N)) * size / (s2 * np.sqrt(K2))).astype(np.float32),
        "w4_words": w4_words, "w4_scales": w4_scales,
    }

def reference(tab_words, tab_scales, offs, tab2_words, tab2_scales, offs2, pos1, w1, w2_words, w2_scales, amp, w5, w3, w4_words, w4_scales):
    v = unpack_weight(tab_words, tab_scales, "e4m3")[:, unstriped(offs)]
    v2 = unpack_weight(tab2_words, tab2_scales, "e4m3")[:, unstriped(offs2)]
    w2 = unpack_weight(w2_words, w2_scales, "e2m1")
    w4 = unpack_weight(w4_words, w4_scales, "e4m3")
    wave = np.sin(mxq(f64(w1), 0, "e4m3").T @ v)
    level = np.tanh(w2.T @ v)
    h = f64(amp)[:, None] * (wave + level)
    reading = mxq(f64(w5), 0, "e4m3").T @ mxq(h, 0, "e4m3")
    left = mxq(f64(w3), 0, "e4m3").T @ v2
    right = w4.T @ v2
    y = np.tanh(reading[:, unstriped(pos1)] + left * right)
    words, scales = planes(y)
    return y, words, scales

@@ -1,0 +1,302 @@
+import math
+from contextlib import ExitStack
+
+import concourse.mybir as mybir
+from concourse.masks import make_identity
+
+K, H, N, S, T, K2, V, TV = 1024, 512, 1024, 1024, 4096, 512, 512, 2048
+FLOPS = 2 * (2 * K * H * S + H * N * S + 2 * K2 * N * V)
+
+F32 = mybir.dt.float32
+BF16 = mybir.dt.bfloat16
+I32 = mybir.dt.int32
+U32 = mybir.dt.uint32
+U16 = mybir.dt.uint16
+U8 = mybir.dt.uint8
+E4M3 = mybir.dt.float8_e4m3fn_x4
+E2M1 = mybir.dt.float4_e2m1fn_x4
+ACT = mybir.ActivationFunctionType
+ALU = mybir.AluOpType
+
+P = 128
+BANK = 512
+
+
+def tile_list_electrode_voxel_features_kernel(
+    tc, tab_words, tab_scales, offs, tab2_words, tab2_scales, offs2, pos1,
+    w1, w2_words, w2_scales, amp, w5, w3, w4_words, w4_scales, out_0, out_1, out_2,
+):
+    nc = tc.nc
+    with ExitStack() as ctx:
+        lists = ctx.enter_context(tc.tile_pool(name="lists", bufs=1))
+        keep = ctx.enter_context(tc.tile_pool(name="keep", bufs=1))
+        dock = ctx.enter_context(tc.tile_pool(name="dock", bufs=1))
+        ring = ctx.enter_context(tc.tile_pool(name="ring", bufs=2))
+        psum = ctx.enter_context(tc.psum_pool(name="psum", bufs=2))
+
+        def held(shape, dtype, name):
+            return keep.tile(shape, dtype, name=name, align_bytes=64)
+
+        def as_words(packed):
+            return packed.rearrange("p c i -> p (c i)").bitcast(I32)
+
+        def zero(tile_ap):
+            nc.vector.memset(tile_ap.bitcast(I32), 0)
+
+        def landing(shape, dtype, name, kib):
+            return dock.tile(shape, dtype, name=name, offset=1024 * kib)
+
+        def reused(shape, dtype, name, tag):
+            return keep.tile(shape, dtype, name=name, tag=tag, align_bytes=64)
+
+        def load_scale_rows(queue, plane, first, rows):
+            count = rows.shape[0] * 4
+            for q in range(4):
+                queue.dma_start(
+                    out=plane[32 * q + first : 32 * q + first + count, :].bitcast(I32),
+                    in_=rows[:, 4 * q : 4 * q + 4, :].bitcast(I32),
+                )
+
+        def load_rows(weight, rows, cols, name, kib):
+            raw = landing([P, 4, BANK], F32, name, kib)
+            nc.sync.dma_start(out=raw[:], in_=weight[rows, cols].rearrange("(p j) c -> p j c", j=4))
+            return raw
+
+        def copy_on(engine, out, in_):
+            if engine == "scalar":
+                nc.scalar.copy(out=out, in_=in_)
+            else:
+                nc.vector.tensor_copy(out=out, in_=in_)
+
+        def quantize(codes, plane, staged):
+            nc.vector.quantize_mx(out=codes.bitcast(E4M3), scales=plane, in_=staged)
+
+        def interleave(engine, raw, name):
+            staged = ring.tile([P, 4 * BANK], BF16, name=name, tag="staged", bufs=2, align_bytes=64)
+            copy_on(
+                engine,
+                staged[:].rearrange("p (c i j) -> p c j i", i=4, j=4),
+                raw[:].rearrange("p j (c i) -> p c j i", i=4),
+            )
+            return staged
+
+        def interleave_dealt(engine, raw, name):
+            staged = ring.tile([P, 4 * BANK], BF16, name=name, tag="staged", bufs=2, align_bytes=64)
+            copy_on(
+                engine,
+                staged[:].rearrange("p (t m j) -> p m j t", t=4, j=4),
+                raw[:].rearrange("p j (m t) -> p m j t", t=4),
+            )
+            return staged
+
+        idx = lists.tile([P, S // 16], U16, name="idx")
+        nc.sync.dma_start(idx[:], offs)
+        idx2 = lists.tile([P, V // 16], U16, name="idx2")
+        nc.sync.dma_start(idx2[:], offs2)
+        place = lists.tile([P, V // 16], U16, name="place")
+        nc.sync.dma_start(place[:], pos1)
+        amp_rows = landing([P, 4], F32, "amp_rows", 16)
+        nc.sync.dma_start(out=amp_rows[:], in_=amp.rearrange("(p t) -> p t", t=4))
+        tab_s = landing([P, T], U8, "tab_s", 32)
+        zero(tab_s[:])
+        w2_s = held([P, 2, H], U8, "w2_s")
+        zero(w2_s[:])
+        tab2_s = held([P, TV], U8, "tab2_s")
+        zero(tab2_s[:])
+        w4_s_raw = held([P, N], U8, "w4_s_raw")
+        zero(w4_s_raw[:])
+        v_s1 = reused([P, S], U8, "v_s1", "e")
+        zero(v_s1[:])
+
+        gain = held([P, P, 4], F32, "gain")
+        nc.vector.tensor_copy(out=gain[:], in_=amp_rows[:].unsqueeze(1).to_broadcast([P, P, 4]))
+        tab = [landing([P, T], I32, f"tab{a}", 16 * a) for a in range(2)]
+        nc.sync.dma_start(out=tab[0][:], in_=as_words(tab_words[0]))
+        w2_w = held([P, 2, 2 * H], U8, "w2_w")
+        nc.sync.dma_start(out=w2_w[:].bitcast(I32), in_=w2_words.bitcast(I32).rearrange("a p c -> p a c"))
+        load_scale_rows(nc.sync, tab_s, 0, tab_scales)
+        nc.sync.dma_start(out=tab[1][:], in_=as_words(tab_words[1]))
+        for q in range(4):
+            nc.gpsimd.dma_start(
+                out=w2_s[32 * q : 32 * q + 4, :, :].bitcast(I32),
+                in_=w2_scales[:, 4 * q : 4 * q + 4, :].bitcast(I32).rearrange("a r c -> r a c"),
+            )
+        load_scale_rows(nc.gpsimd, tab2_s, 8, tab2_scales)
+        load_scale_rows(nc.gpsimd, w4_s_raw, 12, w4_scales)
+
+        ident = held([P, P], F32, "ident")
+        make_identity(nc, ident[:])
+        one = held([P, 1], F32, "one")
+        nc.vector.memset(one[:], 1.0)
+        quarter_pi = held([P, 1], F32, "quarter_pi")
+        nc.vector.tensor_scalar(quarter_pi[:], one[:], math.pi / 4, None, ALU.mult)
+
+        v_w = [[held([P, BANK], U32, f"v_w{a}{half}") for half in range(2)] for a in range(2)]
+
+        def gather_words(a):
+            for half in range(2):
+                nc.vector.tensor_copy(
+                    v_w[a][half][:], tab[a][:].bitcast(U32).indirect(idx[:, 32 * half : 32 * (half + 1)])
+                )
+
+        gather_words(0)
+        w1_raw = [load_rows(w1, slice(0, BANK), slice(0, H), "w1_raw0", 0)]
+        v_s = held([P, S], U8, "v_s")
+        nc.vector.tensor_copy(v_s[:], tab_s[:].indirect(idx[:]))
+        nc.scalar.dma_start(out=v_s1[0:100, :].bitcast(I32), in_=v_s[4:104, :].bitcast(I32))
+        w1_raw.append(load_rows(w1, slice(BANK, K), slice(0, H), "w1_raw1", 32))
+        gather_words(1)
+
+        def v_codes(a, jt):
+            return v_w[a][jt // 4][:, P * (jt % 4) : P * (jt % 4 + 1)].bitcast(E4M3)
+
+        tab2 = landing([P, TV], I32, "tab2", 16)
+        nc.sync.dma_start(out=tab2[:], in_=as_words(tab2_words[0]))
+
+        level = [ring.tile([P, 4, BANK], F32, name=f"level{half}", tag="quad") for half in range(2)]
+        for jt in range(8):
+            cols = slice(P * jt, P * (jt + 1))
+            acc = psum.tile([P, BANK], F32, name=f"z{jt}", tag="first")
+            for a in range(2):
+                nc.tensor.matmul_mx(
+                    out=acc[:], lhsT=v_codes(a, jt), lhsT_scale=(v_s, v_s1)[a][:, cols],
+                    rhs=w2_w[:, a, :].bitcast(E2M1), rhs_scale=w2_s[:, a, :], start=(a == 0), stop=(a == 1),
+                )
+            nc.scalar.activation(
+                out=level[jt // 4][:, jt % 4, :].rearrange("p (t m) -> p t m", t=4),
+                in_=acc[:].rearrange("p (m t) -> p t m", t=4), func=ACT.Tanh,
+            )
+
+        w1_w = [held([P, H], U32, f"w1_w{a}") for a in range(2)]
+        w1_s = [held([P, H], U8, f"w1_s{a}") for a in range(2)]
+        for a in range(2):
+            quantize(w1_w[a][:], w1_s[a][:], interleave("vector", w1_raw[a], f"w1_staged{a}")[:])
+
+        v2_s = held([P, V], U8, "v2_s")
+        v2_w = held([P, V], U32, "v2_w")
+        w4_w = held([P, N], I32, "w4_w")
+        w4_s = reused([P, N], U8, "w4_s", "e")
+        w3_w = [held([P, BANK], U32, f"w3_w{g}") for g in range(2)]
+        w3_s = [held([P, BANK], U8, f"w3_s{g}") for g in range(2)]
+        w5_w = [held([P, BANK], U32, f"w5_w{g}") for g in range(2)]
+        w5_s = [held([P, BANK], U8, f"w5_s{g}") for g in range(2)]
+
+        def gather_voxels():
+            nc.vector.tensor_copy(v2_s[:], tab2_s[:].indirect(idx2[:]))
+            nc.vector.tensor_copy(v2_w[:], tab2[:].bitcast(U32).indirect(idx2[:]))
+
+        def deal_w4():
+            w4_w_raw = landing([P, N], I32, "w4_w_raw", 0)
+            nc.sync.dma_start(out=w4_w_raw[:], in_=as_words(w4_words[0]))
+            nc.vector.tensor_copy(
+                out=w4_w[:].rearrange("p (g t c i) -> p g c t i", g=2, t=4, i=4),
+                in_=w4_w_raw[:].rearrange("p (g c i t) -> p g c t i", g=2, t=4, i=4),
+            )
+            nc.vector.tensor_copy(
+                out=w4_s[:].rearrange("p (g t m) -> p g t m", g=2, t=4),
+                in_=w4_s_raw[:].rearrange("p (g m t) -> p g t m", g=2, t=4),
+            )
+
+        def prepare_w3(g):
+            raw = load_rows(w3, slice(0, K2), slice(BANK * g, BANK * (g + 1)), f"w3_raw{g}", (24, 32)[g])
+            quantize(w3_w[g][:], w3_s[g][:], interleave_dealt("vector", raw, f"w3_staged{g}")[:])
+
+        def prepare_w5(g):
+            raw = load_rows(w5, slice(0, H), slice(BANK * g, BANK * (g + 1)), f"w5_raw{g}", (6, 16)[g])
+            quantize(w5_w[g][:], w5_s[g][:], interleave_dealt("scalar", raw, f"w5_staged{g}")[:])
+
+        beside = {0: gather_voxels, 1: lambda: prepare_w3(0), 2: deal_w4, 4: lambda: prepare_w5(0),
+                  5: lambda: prepare_w3(1), 7: lambda: prepare_w5(1)}
+
+        h_w = [held([P, BANK], U32, f"h_w{half}") for half in range(2)]
+        h_s = [held([P, BANK], U8, f"h_s{half}") for half in range(2)]
+        for jt in range(8):
+            cols = slice(P * jt, P * (jt + 1))
+            acc = psum.tile([P, BANK], F32, name=f"x{jt}", tag="first")
+            for a in range(2):
+                nc.tensor.matmul_mx(
+                    out=acc[:], lhsT=v_codes(a, jt), lhsT_scale=v_s[4 * a :, cols],
+                    rhs=w1_w[a][:].bitcast(E4M3), rhs_scale=w1_s[a][:], start=(a == 0), stop=(a == 1),
+                )
+            sine = ring.tile([P, BANK], F32, name=f"sine{jt}", tag="sine")
+            nc.scalar.activation(
+                out=sine[:].rearrange("p (t m) -> p t m", t=4),
+                in_=acc[:].rearrange("p (m t) -> p t m", t=4),
+                func=ACT.Sin, scale=0.5, bias=quarter_pi[:],
+            )
+            lifted = ring.tile([P, BANK], F32, name=f"lifted{jt}", tag="lifted", bufs=3)
+            if jt in ():
+                nc.vector.scalar_tensor_tensor(lifted[:], sine[:], 2.0, sine[:], ALU.mult, ALU.mult)
+            else:
+                nc.scalar.activation(out=lifted[:], in_=sine[:], func=ACT.Square, scale=math.sqrt(2.0))
+            turned = psum.tile([P, 4, P], F32, name=f"turned{jt}", tag="turned")
+            for t in range(4):
+                nc.tensor.matmul(turned[:, t, :], level[jt // 4][:, jt % 4, P * t : P * (t + 1)], ident[:],
+                                 start=(t == 0), stop=False, is_transpose=True)
+            for t in range(4):
+                nc.tensor.matmul(turned[:, t, :], lifted[:, P * t : P * (t + 1)], ident[:],
+                                 start=False, stop=(t == 3), is_transpose=True)
+            if jt % 2 == 0:
+                h_staged = ring.tile([P, 2 * BANK], BF16, name=f"h_staged{jt}", tag="h_staged", align_bytes=64)
+            nc.vector.scalar_tensor_tensor(
+                h_staged[:, BANK * (jt % 2) : BANK * (jt % 2 + 1)].rearrange("p (j t) -> p j t", t=4),
+                turned[:].rearrange("p t j -> p j t"), 1.0,
+                gain[:], ALU.subtract, ALU.mult,
+            )
+            if jt % 2 == 1:
+                pair = slice(P * (jt % 4 - 1), P * (jt % 4 + 1))
+                quantize(h_w[jt // 4][:, pair], h_s[jt // 4][:, pair], h_staged[:])
+
+            if jt in beside:
+                beside[jt]()
+
+        y_s = held([P, 2, V], U8, "y_s")
+        rows_out = out_0.rearrange("(g p t) j -> g t p j", g=2, t=4)
+
+        def products(g, t):
+            part = slice(P * t, P * (t + 1))
+            wide = slice(BANK * g + P * t, BANK * g + P * (t + 1))
+            left = psum.tile([P, V], F32, name=f"left{g}{t}", tag="left", bufs=1)
+            nc.tensor.matmul_mx(
+                out=left[:], lhsT=w3_w[g][:, part].bitcast(E4M3), lhsT_scale=w3_s[g][:, part],
+                rhs=v2_w[:].bitcast(E4M3), rhs_scale=v2_s[8:, :], start=True, stop=True,
+            )
+            right = psum.tile([P, V], F32, name=f"right{g}{t}", tag="right", bufs=1)
+            nc.tensor.matmul_mx(
+                out=right[:], lhsT=w4_w[:, wide].bitcast(E4M3), lhsT_scale=w4_s[12:, wide],
+                rhs=v2_w[:].bitcast(E4M3), rhs_scale=v2_s[8:, :], start=True, stop=True,
+            )
+            left_sb = ring.tile([P, V], F32, name=f"left_sb{g}{t}", tag="left_sb")
+            nc.scalar.copy(out=left_sb[:], in_=left[:])
+            both = ring.tile([P, V], F32, name=f"both{g}{t}", tag="both", bufs=8)
+            nc.vector.tensor_tensor(both[:], right[:], left_sb[:], ALU.mult)
+            reading = ring.tile([P, S], F32, name=f"reading{g}{t}", tag="reading", bufs=8)
+            for half in range(2):
+                acc = psum.tile([P, BANK], F32, name=f"r{g}{t}{half}",
+                                tag=("second", ("first", "turned")[t % 2])[half])
+                nc.tensor.matmul_mx(
+                    out=acc[:], lhsT=w5_w[g][:, part].bitcast(E4M3), lhsT_scale=w5_s[g][:, part],
+                    rhs=h_w[half][:].bitcast(E4M3), rhs_scale=h_s[half][:], start=True, stop=True,
+                )
+                nc.scalar.copy(out=reading[:, BANK * half : BANK * (half + 1)], in_=acc[:])
+            return reading, both
+
+        made = [products(0, 0)]
+        for g in range(2):
+            y = ring.tile([P, 4, V], F32, name=f"y{g}", tag="quad")
+            for t in range(4):
+                if 4 * g + t + 1 < 8:
+                    made.append(products(*divmod(4 * g + t + 1, 4)))
+                reading, both = made[4 * g + t]
+                total = ring.tile([P, V], F32, name=f"total{g}{t}", tag="total", bufs=3)
+                nc.vector.tensor_tensor(total[:], reading[:].indirect(place[:]), both[:], ALU.add)
+                nc.scalar.activation(out=y[:, t, :], in_=total[:], func=ACT.Tanh)
+                nc.sync.dma_start(out=rows_out[g, t], in_=y[:, t, :])
+            y_w = held([P, V], U32, f"y_w{g}")
+            quantize(y_w[:], y_s[:, g, :], interleave("vector", y, f"y_staged{g}")[:])
+            nc.sync.dma_start(out=as_words(out_1[g]), in_=y_w[:].bitcast(I32))
+        for q in range(4):
+            nc.sync.dma_start(
+                out=out_2[:, 4 * q : 4 * q + 4, :].bitcast(I32).rearrange("g r c -> r g c"),
+                in_=y_s[32 * q : 32 * q + 4, :, :].bitcast(I32),
+            )

@@ -32,10 +32,13 @@ def tile_list_electrode_voxel_features_kernel(
         keep = ctx.enter_context(tc.tile_pool(name="keep", bufs=1))
         dock = ctx.enter_context(tc.tile_pool(name="dock", bufs=1))
         ring = ctx.enter_context(tc.tile_pool(name="ring", bufs=2))
-        psum = ctx.enter_context(tc.psum_pool(name="psum", bufs=2))
+        psum = ctx.enter_context(tc.psum_pool(name="psum", bufs=1))
 
         def held(shape, dtype, name):
             return keep.tile(shape, dtype, name=name, align_bytes=64)
+
+        def bank(number, shape, name):
+            return psum.tile(shape, F32, name=name, tag=f"bank{number}")
 
         def as_words(packed):
             return packed.rearrange("p c i -> p (c i)").bitcast(I32)
@@ -44,10 +47,7 @@ def tile_list_electrode_voxel_features_kernel(
             nc.vector.memset(tile_ap.bitcast(I32), 0)
 
         def landing(shape, dtype, name, kib):
-            return dock.tile(shape, dtype, name=name, offset=1024 * kib)
-
-        def reused(shape, dtype, name, tag):
-            return keep.tile(shape, dtype, name=name, tag=tag, align_bytes=64)
+            return dock.tile(shape, dtype, name=name, offset=1024 * kib, align_bytes=64)
 
         def load_scale_rows(queue, plane, first, rows):
             count = rows.shape[0] * 4
@@ -70,15 +70,6 @@ def tile_list_electrode_voxel_features_kernel(
 
         def quantize(codes, plane, staged):
             nc.vector.quantize_mx(out=codes.bitcast(E4M3), scales=plane, in_=staged)
-
-        def interleave(engine, raw, name):
-            staged = ring.tile([P, 4 * BANK], BF16, name=name, tag="staged", bufs=2, align_bytes=64)
-            copy_on(
-                engine,
-                staged[:].rearrange("p (c i j) -> p c j i", i=4, j=4),
-                raw[:].rearrange("p j (c i) -> p c j i", i=4),
-            )
-            return staged
 
         def interleave_dealt(engine, raw, name):
             staged = ring.tile([P, 4 * BANK], BF16, name=name, tag="staged", bufs=2, align_bytes=64)
@@ -105,7 +96,7 @@ def tile_list_electrode_voxel_features_kernel(
         zero(tab2_s[:])
         w4_s_raw = held([P, N], U8, "w4_s_raw")
         zero(w4_s_raw[:])
-        v_s1 = reused([P, S], U8, "v_s1", "e")
+        v_s1 = held([P, S], U8, "v_s1")
         zero(v_s1[:])
 
         gain = held([P, P, 4], F32, "gain")
@@ -156,30 +147,31 @@ def tile_list_electrode_voxel_features_kernel(
         level = [ring.tile([P, 4, BANK], F32, name=f"level{half}", tag="quad") for half in range(2)]
         for jt in range(8):
             cols = slice(P * jt, P * (jt + 1))
-            acc = psum.tile([P, BANK], F32, name=f"z{jt}", tag="first")
+            acc = bank(jt % 4, [P, BANK], f"z{jt}")
             for a in range(2):
                 nc.tensor.matmul_mx(
                     out=acc[:], lhsT=v_codes(a, jt), lhsT_scale=(v_s, v_s1)[a][:, cols],
                     rhs=w2_w[:, a, :].bitcast(E2M1), rhs_scale=w2_s[:, a, :], start=(a == 0), stop=(a == 1),
                 )
             nc.scalar.activation(
-                out=level[jt // 4][:, jt % 4, :].rearrange("p (t m) -> p t m", t=4),
-                in_=acc[:].rearrange("p (m t) -> p t m", t=4), func=ACT.Tanh,
+                out=level[jt // 4][:, jt % 4, :].rearrange("p (t m) -> p m t", t=4),
+                in_=acc[:].rearrange("p (m t) -> p m t", t=4), func=ACT.Tanh,
             )
 
         w1_w = [held([P, H], U32, f"w1_w{a}") for a in range(2)]
         w1_s = [held([P, H], U8, f"w1_s{a}") for a in range(2)]
         for a in range(2):
-            quantize(w1_w[a][:], w1_s[a][:], interleave("vector", w1_raw[a], f"w1_staged{a}")[:])
+            quantize(w1_w[a][:], w1_s[a][:], interleave_dealt("vector", w1_raw[a], f"w1_staged{a}")[:])
 
-        v2_s = held([P, V], U8, "v2_s")
         v2_w = held([P, V], U32, "v2_w")
+        v2_s = landing([P, V], U8, "v2_s", 4)
         w4_w = held([P, N], I32, "w4_w")
-        w4_s = reused([P, N], U8, "w4_s", "e")
         w3_w = [held([P, BANK], U32, f"w3_w{g}") for g in range(2)]
         w3_s = [held([P, BANK], U8, f"w3_s{g}") for g in range(2)]
         w5_w = [held([P, BANK], U32, f"w5_w{g}") for g in range(2)]
         w5_s = [held([P, BANK], U8, f"w5_s{g}") for g in range(2)]
+
+        w4_s = []
 
         def gather_voxels():
             nc.vector.tensor_copy(v2_s[:], tab2_s[:].indirect(idx2[:]))
@@ -192,8 +184,9 @@ def tile_list_electrode_voxel_features_kernel(
                 out=w4_w[:].rearrange("p (g t c i) -> p g c t i", g=2, t=4, i=4),
                 in_=w4_w_raw[:].rearrange("p (g c i t) -> p g c t i", g=2, t=4, i=4),
             )
+            w4_s.append(landing([P, N], U8, "w4_s", 24))
             nc.vector.tensor_copy(
-                out=w4_s[:].rearrange("p (g t m) -> p g t m", g=2, t=4),
+                out=w4_s[0][:].rearrange("p (g t m) -> p g t m", g=2, t=4),
                 in_=w4_s_raw[:].rearrange("p (g m t) -> p g t m", g=2, t=4),
             )
 
@@ -203,7 +196,7 @@ def tile_list_electrode_voxel_features_kernel(
 
         def prepare_w5(g):
             raw = load_rows(w5, slice(0, H), slice(BANK * g, BANK * (g + 1)), f"w5_raw{g}", (6, 16)[g])
-            quantize(w5_w[g][:], w5_s[g][:], interleave_dealt("scalar", raw, f"w5_staged{g}")[:])
+            quantize(w5_w[g][:], w5_s[g][:], interleave_dealt(("scalar", "scalar")[g], raw, f"w5_staged{g}")[:])
 
         beside = {0: gather_voxels, 1: lambda: prepare_w3(0), 2: deal_w4, 4: lambda: prepare_w5(0),
                   5: lambda: prepare_w3(1), 7: lambda: prepare_w5(1)}
@@ -212,7 +205,7 @@ def tile_list_electrode_voxel_features_kernel(
         h_s = [held([P, BANK], U8, f"h_s{half}") for half in range(2)]
         for jt in range(8):
             cols = slice(P * jt, P * (jt + 1))
-            acc = psum.tile([P, BANK], F32, name=f"x{jt}", tag="first")
+            acc = bank(jt % 4, [P, BANK], f"x{jt}")
             for a in range(2):
                 nc.tensor.matmul_mx(
                     out=acc[:], lhsT=v_codes(a, jt), lhsT_scale=v_s[4 * a :, cols],
@@ -220,16 +213,14 @@ def tile_list_electrode_voxel_features_kernel(
                 )
             sine = ring.tile([P, BANK], F32, name=f"sine{jt}", tag="sine")
             nc.scalar.activation(
-                out=sine[:].rearrange("p (t m) -> p t m", t=4),
-                in_=acc[:].rearrange("p (m t) -> p t m", t=4),
-                func=ACT.Sin, scale=0.5, bias=quarter_pi[:],
+                out=sine[:], in_=acc[:], func=ACT.Sin, scale=0.5, bias=quarter_pi[:],
             )
             lifted = ring.tile([P, BANK], F32, name=f"lifted{jt}", tag="lifted", bufs=3)
             if jt in ():
                 nc.vector.scalar_tensor_tensor(lifted[:], sine[:], 2.0, sine[:], ALU.mult, ALU.mult)
             else:
                 nc.scalar.activation(out=lifted[:], in_=sine[:], func=ACT.Square, scale=math.sqrt(2.0))
-            turned = psum.tile([P, 4, P], F32, name=f"turned{jt}", tag="turned")
+            turned = bank(4 + jt % 2, [P, 4, P], f"turned{jt}")
             for t in range(4):
                 nc.tensor.matmul(turned[:, t, :], level[jt // 4][:, jt % 4, P * t : P * (t + 1)], ident[:],
                                  start=(t == 0), stop=False, is_transpose=True)
@@ -256,14 +247,14 @@ def tile_list_electrode_voxel_features_kernel(
         def products(g, t):
             part = slice(P * t, P * (t + 1))
             wide = slice(BANK * g + P * t, BANK * g + P * (t + 1))
-            left = psum.tile([P, V], F32, name=f"left{g}{t}", tag="left", bufs=1)
+            left = bank(6, [P, V], f"left{g}{t}")
             nc.tensor.matmul_mx(
                 out=left[:], lhsT=w3_w[g][:, part].bitcast(E4M3), lhsT_scale=w3_s[g][:, part],
                 rhs=v2_w[:].bitcast(E4M3), rhs_scale=v2_s[8:, :], start=True, stop=True,
             )
-            right = psum.tile([P, V], F32, name=f"right{g}{t}", tag="right", bufs=1)
+            right = bank(7, [P, V], f"right{g}{t}")
             nc.tensor.matmul_mx(
-                out=right[:], lhsT=w4_w[:, wide].bitcast(E4M3), lhsT_scale=w4_s[12:, wide],
+                out=right[:], lhsT=w4_w[:, wide].bitcast(E4M3), lhsT_scale=w4_s[0][12:, wide],
                 rhs=v2_w[:].bitcast(E4M3), rhs_scale=v2_s[8:, :], start=True, stop=True,
             )
             left_sb = ring.tile([P, V], F32, name=f"left_sb{g}{t}", tag="left_sb")
@@ -272,8 +263,7 @@ def tile_list_electrode_voxel_features_kernel(
             nc.vector.tensor_tensor(both[:], right[:], left_sb[:], ALU.mult)
             reading = ring.tile([P, S], F32, name=f"reading{g}{t}", tag="reading", bufs=8)
             for half in range(2):
-                acc = psum.tile([P, BANK], F32, name=f"r{g}{t}{half}",
-                                tag=("second", ("first", "turned")[t % 2])[half])
+                acc = bank((2 * (4 * g + t) + half) % 6, [P, BANK], f"r{g}{t}{half}")
                 nc.tensor.matmul_mx(
                     out=acc[:], lhsT=w5_w[g][:, part].bitcast(E4M3), lhsT_scale=w5_s[g][:, part],
                     rhs=h_w[half][:].bitcast(E4M3), rhs_scale=h_s[half][:], start=True, stop=True,
@@ -284,19 +274,32 @@ def tile_list_electrode_voxel_features_kernel(
         made = [products(0, 0)]
         for g in range(2):
             y = ring.tile([P, 4, V], F32, name=f"y{g}", tag="quad")
+            y_w = held([P, V], U32, f"y_w{g}")
             for t in range(4):
                 if 4 * g + t + 1 < 8:
                     made.append(products(*divmod(4 * g + t + 1, 4)))
                 reading, both = made[4 * g + t]
-                total = ring.tile([P, V], F32, name=f"total{g}{t}", tag="total", bufs=3)
-                nc.vector.tensor_tensor(total[:], reading[:].indirect(place[:]), both[:], ALU.add)
-                nc.scalar.activation(out=y[:, t, :], in_=total[:], func=ACT.Tanh)
+                pieces = 2 if (g, t) == (1, 3) else 1
+                width = V // pieces
+                for piece in range(pieces):
+                    cols = slice(width * piece, width * (piece + 1))
+                    total = ring.tile([P, width], F32, name=f"total{g}{t}{piece}", tag="total", bufs=3)
+                    listed = place[:, width // 16 * piece : width // 16 * (piece + 1)]
+                    nc.vector.tensor_tensor(total[:], reading[:].indirect(listed), both[:, cols], ALU.add)
+                    nc.scalar.activation(out=y[:, t, cols], in_=total[:], func=ACT.Tanh)
                 nc.sync.dma_start(out=rows_out[g, t], in_=y[:, t, :])
-            y_w = held([P, V], U32, f"y_w{g}")
-            quantize(y_w[:], y_s[:, g, :], interleave("vector", y, f"y_staged{g}")[:])
-            nc.sync.dma_start(out=as_words(out_1[g]), in_=y_w[:].bitcast(I32))
+            for piece in range(pieces):
+                cols = slice(width * piece, width * (piece + 1))
+                staged = ring.tile([P, 4 * width], BF16, name=f"y_staged{g}{piece}", tag="staged", bufs=2, align_bytes=64)
+                copy_on(
+                    "vector",
+                    staged[:].rearrange("p (c i j) -> p c j i", i=4, j=4),
+                    y[:, :, cols].rearrange("p j (c i) -> p c j i", i=4),
+                )
+                quantize(y_w[:, cols], y_s[:, g, cols], staged[:])
+                nc.sync.dma_start(out=as_words(out_1[g])[:, cols], in_=y_w[:, cols].bitcast(I32))
         for q in range(4):
-            nc.sync.dma_start(
+            nc.scalar.dma_start(
                 out=out_2[:, 4 * q : 4 * q + 4, :].bitcast(I32).rearrange("g r c -> r g c"),
                 in_=y_s[32 * q : 32 * q + 4, :, :].bitcast(I32),
             )

@@ -122,6 +122,8 @@ def tile_list_electrode_voxel_features_kernel(
         quarter_pi = held([P, 1], F32, "quarter_pi")
         nc.vector.tensor_scalar(quarter_pi[:], one[:], math.pi / 4, None, ALU.mult)
 
+        scratch = held([P, 1], F32, "scratch")
+        nc.scalar.activation(out=scratch[:], in_=one[:], func=ACT.Silu)
         v_w = [[held([P, BANK], U32, f"v_w{a}{half}") for half in range(2)] for a in range(2)]
 
         def gather_words(a):

import math
from contextlib import ExitStack

import concourse.mybir as mybir
from concourse.masks import make_identity

K, H, N, S, T, K2, V, TV = 1024, 512, 1024, 1024, 4096, 512, 512, 2048
FLOPS = 2 * (2 * K * H * S + H * N * S + 2 * K2 * N * V)

F32 = mybir.dt.float32
BF16 = mybir.dt.bfloat16
I32 = mybir.dt.int32
U32 = mybir.dt.uint32
U16 = mybir.dt.uint16
U8 = mybir.dt.uint8
E4M3 = mybir.dt.float8_e4m3fn_x4
E2M1 = mybir.dt.float4_e2m1fn_x4
ACT = mybir.ActivationFunctionType
ALU = mybir.AluOpType

P = 128
BANK = 512


def tile_list_electrode_voxel_features_kernel(
    tc, tab_words, tab_scales, offs, tab2_words, tab2_scales, offs2, pos1,
    w1, w2_words, w2_scales, amp, w5, w3, w4_words, w4_scales, out_0, out_1, out_2,
):
    nc = tc.nc
    with ExitStack() as ctx:
        lists = ctx.enter_context(tc.tile_pool(name="lists", bufs=1))
        keep = ctx.enter_context(tc.tile_pool(name="keep", bufs=1))
        dock = ctx.enter_context(tc.tile_pool(name="dock", bufs=1))
        ring = ctx.enter_context(tc.tile_pool(name="ring", bufs=2))
        psum = ctx.enter_context(tc.psum_pool(name="psum", bufs=1))

        def held(shape, dtype, name):
            return keep.tile(shape, dtype, name=name, align_bytes=64)

        def bank(number, shape, name):
            return psum.tile(shape, F32, name=name, tag=f"bank{number}")

        def as_words(packed):
            return packed.rearrange("p c i -> p (c i)").bitcast(I32)

        def zero(tile_ap):
            nc.vector.memset(tile_ap.bitcast(I32), 0)

        def landing(shape, dtype, name, kib):
            return dock.tile(shape, dtype, name=name, offset=1024 * kib, align_bytes=64)

        def load_scale_rows(queue, plane, first, rows):
            count = rows.shape[0] * 4
            for q in range(4):
                queue.dma_start(
                    out=plane[32 * q + first : 32 * q + first + count, :].bitcast(I32),
                    in_=rows[:, 4 * q : 4 * q + 4, :].bitcast(I32),
                )

        def load_rows(weight, rows, cols, name, kib):
            raw = landing([P, 4, BANK], F32, name, kib)
            nc.sync.dma_start(out=raw[:], in_=weight[rows, cols].rearrange("(p j) c -> p j c", j=4))
            return raw

        def copy_on(engine, out, in_):
            if engine == "scalar":
                nc.scalar.copy(out=out, in_=in_)
            else:
                nc.vector.tensor_copy(out=out, in_=in_)

        def quantize(codes, plane, staged):
            nc.vector.quantize_mx(out=codes.bitcast(E4M3), scales=plane, in_=staged)

        def interleave_dealt(engine, raw, name):
            staged = ring.tile([P, 4 * BANK], BF16, name=name, tag="staged", bufs=2, align_bytes=64)
            copy_on(
                engine,
                staged[:].rearrange("p (t m j) -> p m j t", t=4, j=4),
                raw[:].rearrange("p j (m t) -> p m j t", t=4),
            )
            return staged

        idx = lists.tile([P, S // 16], U16, name="idx")
        nc.sync.dma_start(idx[:], offs)
        idx2 = lists.tile([P, V // 16], U16, name="idx2")
        nc.sync.dma_start(idx2[:], offs2)
        place = lists.tile([P, V // 16], U16, name="place")
        nc.sync.dma_start(place[:], pos1)
        amp_rows = landing([P, 4], F32, "amp_rows", 16)
        nc.sync.dma_start(out=amp_rows[:], in_=amp.rearrange("(p t) -> p t", t=4))
        tab_s = landing([P, T], U8, "tab_s", 32)
        zero(tab_s[:])
        w2_s = held([P, 2, H], U8, "w2_s")
        zero(w2_s[:])
        tab2_s = held([P, TV], U8, "tab2_s")
        zero(tab2_s[:])
        w4_s_raw = held([P, N], U8, "w4_s_raw")
        zero(w4_s_raw[:])
        v_s1 = held([P, S], U8, "v_s1")
        zero(v_s1[:])

        gain = held([P, P, 4], F32, "gain")
        nc.vector.tensor_copy(out=gain[:], in_=amp_rows[:].unsqueeze(1).to_broadcast([P, P, 4]))
        tab = [landing([P, T], I32, f"tab{a}", 16 * a) for a in range(2)]
        nc.sync.dma_start(out=tab[0][:], in_=as_words(tab_words[0]))
        w2_w = held([P, 2, 2 * H], U8, "w2_w")
        nc.sync.dma_start(out=w2_w[:].bitcast(I32), in_=w2_words.bitcast(I32).rearrange("a p c -> p a c"))
        load_scale_rows(nc.sync, tab_s, 0, tab_scales)
        nc.sync.dma_start(out=tab[1][:], in_=as_words(tab_words[1]))
        for q in range(4):
            nc.gpsimd.dma_start(
                out=w2_s[32 * q : 32 * q + 4, :, :].bitcast(I32),
                in_=w2_scales[:, 4 * q : 4 * q + 4, :].bitcast(I32).rearrange("a r c -> r a c"),
            )
        load_scale_rows(nc.gpsimd, tab2_s, 8, tab2_scales)
        load_scale_rows(nc.gpsimd, w4_s_raw, 12, w4_scales)

        ident = held([P, P], F32, "ident")
        make_identity(nc, ident[:])
        one = held([P, 1], F32, "one")
        nc.vector.memset(one[:], 1.0)
        quarter_pi = held([P, 1], F32, "quarter_pi")
        nc.vector.tensor_scalar(quarter_pi[:], one[:], math.pi / 4, None, ALU.mult)

        scratch = held([P, 1], F32, "scratch")
        nc.scalar.activation(out=scratch[:], in_=one[:], func=ACT.Silu)
        v_w = [[held([P, BANK], U32, f"v_w{a}{half}") for half in range(2)] for a in range(2)]

        def gather_words(a):
            for half in range(2):
                nc.vector.tensor_copy(
                    v_w[a][half][:], tab[a][:].bitcast(U32).indirect(idx[:, 32 * half : 32 * (half + 1)])
                )

        gather_words(0)
        w1_raw = [load_rows(w1, slice(0, BANK), slice(0, H), "w1_raw0", 0)]
        v_s = held([P, S], U8, "v_s")
        nc.vector.tensor_copy(v_s[:], tab_s[:].indirect(idx[:]))
        nc.scalar.dma_start(out=v_s1[0:100, :].bitcast(I32), in_=v_s[4:104, :].bitcast(I32))
        w1_raw.append(load_rows(w1, slice(BANK, K), slice(0, H), "w1_raw1", 32))
        gather_words(1)

        def v_codes(a, jt):
            return v_w[a][jt // 4][:, P * (jt % 4) : P * (jt % 4 + 1)].bitcast(E4M3)

        tab2 = landing([P, TV], I32, "tab2", 16)
        nc.sync.dma_start(out=tab2[:], in_=as_words(tab2_words[0]))

        level = [ring.tile([P, 4, BANK], F32, name=f"level{half}", tag="quad") for half in range(2)]
        for jt in range(8):
            cols = slice(P * jt, P * (jt + 1))
            acc = bank(jt % 4, [P, BANK], f"z{jt}")
            for a in range(2):
                nc.tensor.matmul_mx(
                    out=acc[:], lhsT=v_codes(a, jt), lhsT_scale=(v_s, v_s1)[a][:, cols],
                    rhs=w2_w[:, a, :].bitcast(E2M1), rhs_scale=w2_s[:, a, :], start=(a == 0), stop=(a == 1),
                )
            nc.scalar.activation(
                out=level[jt // 4][:, jt % 4, :].rearrange("p (t m) -> p m t", t=4),
                in_=acc[:].rearrange("p (m t) -> p m t", t=4), func=ACT.Tanh,
            )

        w1_w = [held([P, H], U32, f"w1_w{a}") for a in range(2)]
        w1_s = [held([P, H], U8, f"w1_s{a}") for a in range(2)]
        for a in range(2):
            quantize(w1_w[a][:], w1_s[a][:], interleave_dealt("vector", w1_raw[a], f"w1_staged{a}")[:])

        v2_w = held([P, V], U32, "v2_w")
        v2_s = landing([P, V], U8, "v2_s", 4)
        w4_w = held([P, N], I32, "w4_w")
        w3_w = [held([P, BANK], U32, f"w3_w{g}") for g in range(2)]
        w3_s = [held([P, BANK], U8, f"w3_s{g}") for g in range(2)]
        w5_w = [held([P, BANK], U32, f"w5_w{g}") for g in range(2)]
        w5_s = [held([P, BANK], U8, f"w5_s{g}") for g in range(2)]

        w4_s = []

        def gather_voxels():
            nc.vector.tensor_copy(v2_s[:], tab2_s[:].indirect(idx2[:]))
            nc.vector.tensor_copy(v2_w[:], tab2[:].bitcast(U32).indirect(idx2[:]))

        def deal_w4():
            w4_w_raw = landing([P, N], I32, "w4_w_raw", 0)
            nc.sync.dma_start(out=w4_w_raw[:], in_=as_words(w4_words[0]))
            nc.vector.tensor_copy(
                out=w4_w[:].rearrange("p (g t c i) -> p g c t i", g=2, t=4, i=4),
                in_=w4_w_raw[:].rearrange("p (g c i t) -> p g c t i", g=2, t=4, i=4),
            )
            w4_s.append(landing([P, N], U8, "w4_s", 24))
            nc.vector.tensor_copy(
                out=w4_s[0][:].rearrange("p (g t m) -> p g t m", g=2, t=4),
                in_=w4_s_raw[:].rearrange("p (g m t) -> p g t m", g=2, t=4),
            )

        def prepare_w3(g):
            raw = load_rows(w3, slice(0, K2), slice(BANK * g, BANK * (g + 1)), f"w3_raw{g}", (24, 32)[g])
            quantize(w3_w[g][:], w3_s[g][:], interleave_dealt("vector", raw, f"w3_staged{g}")[:])

        def prepare_w5(g):
            raw = load_rows(w5, slice(0, H), slice(BANK * g, BANK * (g + 1)), f"w5_raw{g}", (6, 16)[g])
            quantize(w5_w[g][:], w5_s[g][:], interleave_dealt(("scalar", "scalar")[g], raw, f"w5_staged{g}")[:])

        beside = {0: gather_voxels, 1: lambda: prepare_w3(0), 2: deal_w4, 4: lambda: prepare_w5(0),
                  5: lambda: prepare_w3(1), 7: lambda: prepare_w5(1)}

        h_w = [held([P, BANK], U32, f"h_w{half}") for half in range(2)]
        h_s = [held([P, BANK], U8, f"h_s{half}") for half in range(2)]
        for jt in range(8):
            cols = slice(P * jt, P * (jt + 1))
            acc = bank(jt % 4, [P, BANK], f"x{jt}")
            for a in range(2):
                nc.tensor.matmul_mx(
                    out=acc[:], lhsT=v_codes(a, jt), lhsT_scale=v_s[4 * a :, cols],
                    rhs=w1_w[a][:].bitcast(E4M3), rhs_scale=w1_s[a][:], start=(a == 0), stop=(a == 1),
                )
            sine = ring.tile([P, BANK], F32, name=f"sine{jt}", tag="sine")
            nc.scalar.activation(
                out=sine[:], in_=acc[:], func=ACT.Sin, scale=0.5, bias=quarter_pi[:],
            )
            lifted = ring.tile([P, BANK], F32, name=f"lifted{jt}", tag="lifted", bufs=3)
            if jt in ():
                nc.vector.scalar_tensor_tensor(lifted[:], sine[:], 2.0, sine[:], ALU.mult, ALU.mult)
            else:
                nc.scalar.activation(out=lifted[:], in_=sine[:], func=ACT.Square, scale=math.sqrt(2.0))
            turned = bank(4 + jt % 2, [P, 4, P], f"turned{jt}")
            for t in range(4):
                nc.tensor.matmul(turned[:, t, :], level[jt // 4][:, jt % 4, P * t : P * (t + 1)], ident[:],
                                 start=(t == 0), stop=False, is_transpose=True)
            for t in range(4):
                nc.tensor.matmul(turned[:, t, :], lifted[:, P * t : P * (t + 1)], ident[:],
                                 start=False, stop=(t == 3), is_transpose=True)
            if jt % 2 == 0:
                h_staged = ring.tile([P, 2 * BANK], BF16, name=f"h_staged{jt}", tag="h_staged", align_bytes=64)
            nc.vector.scalar_tensor_tensor(
                h_staged[:, BANK * (jt % 2) : BANK * (jt % 2 + 1)].rearrange("p (j t) -> p j t", t=4),
                turned[:].rearrange("p t j -> p j t"), 1.0,
                gain[:], ALU.subtract, ALU.mult,
            )
            if jt % 2 == 1:
                pair = slice(P * (jt % 4 - 1), P * (jt % 4 + 1))
                quantize(h_w[jt // 4][:, pair], h_s[jt // 4][:, pair], h_staged[:])

            if jt in beside:
                beside[jt]()

        y_s = held([P, 2, V], U8, "y_s")
        rows_out = out_0.rearrange("(g p t) j -> g t p j", g=2, t=4)

        def products(g, t):
            part = slice(P * t, P * (t + 1))
            wide = slice(BANK * g + P * t, BANK * g + P * (t + 1))
            left = bank(6, [P, V], f"left{g}{t}")
            nc.tensor.matmul_mx(
                out=left[:], lhsT=w3_w[g][:, part].bitcast(E4M3), lhsT_scale=w3_s[g][:, part],
                rhs=v2_w[:].bitcast(E4M3), rhs_scale=v2_s[8:, :], start=True, stop=True,
            )
            right = bank(7, [P, V], f"right{g}{t}")
            nc.tensor.matmul_mx(
                out=right[:], lhsT=w4_w[:, wide].bitcast(E4M3), lhsT_scale=w4_s[0][12:, wide],
                rhs=v2_w[:].bitcast(E4M3), rhs_scale=v2_s[8:, :], start=True, stop=True,
            )
            left_sb = ring.tile([P, V], F32, name=f"left_sb{g}{t}", tag="left_sb")
            nc.scalar.copy(out=left_sb[:], in_=left[:])
            both = ring.tile([P, V], F32, name=f"both{g}{t}", tag="both", bufs=8)
            nc.vector.tensor_tensor(both[:], right[:], left_sb[:], ALU.mult)
            reading = ring.tile([P, S], F32, name=f"reading{g}{t}", tag="reading", bufs=8)
            for half in range(2):
                acc = bank((2 * (4 * g + t) + half) % 6, [P, BANK], f"r{g}{t}{half}")
                nc.tensor.matmul_mx(
                    out=acc[:], lhsT=w5_w[g][:, part].bitcast(E4M3), lhsT_scale=w5_s[g][:, part],
                    rhs=h_w[half][:].bitcast(E4M3), rhs_scale=h_s[half][:], start=True, stop=True,
                )
                nc.scalar.copy(out=reading[:, BANK * half : BANK * (half + 1)], in_=acc[:])
            return reading, both

        made = [products(0, 0)]
        for g in range(2):
            y = ring.tile([P, 4, V], F32, name=f"y{g}", tag="quad")
            y_w = held([P, V], U32, f"y_w{g}")
            for t in range(4):
                if 4 * g + t + 1 < 8:
                    made.append(products(*divmod(4 * g + t + 1, 4)))
                reading, both = made[4 * g + t]
                pieces = 2 if (g, t) == (1, 3) else 1
                width = V // pieces
                for piece in range(pieces):
                    cols = slice(width * piece, width * (piece + 1))
                    total = ring.tile([P, width], F32, name=f"total{g}{t}{piece}", tag="total", bufs=3)
                    listed = place[:, width // 16 * piece : width // 16 * (piece + 1)]
                    nc.vector.tensor_tensor(total[:], reading[:].indirect(listed), both[:, cols], ALU.add)
                    nc.scalar.activation(out=y[:, t, cols], in_=total[:], func=ACT.Tanh)
                nc.sync.dma_start(out=rows_out[g, t], in_=y[:, t, :])
            for piece in range(pieces):
                cols = slice(width * piece, width * (piece + 1))
                staged = ring.tile([P, 4 * width], BF16, name=f"y_staged{g}{piece}", tag="staged", bufs=2, align_bytes=64)
                copy_on(
                    "vector",
                    staged[:].rearrange("p (c i j) -> p c j i", i=4, j=4),
                    y[:, :, cols].rearrange("p j (c i) -> p c j i", i=4),
                )
                quantize(y_w[:, cols], y_s[:, g, cols], staged[:])
                nc.sync.dma_start(out=as_words(out_1[g])[:, cols], in_=y_w[:, cols].bitcast(I32))
        for q in range(4):
            nc.scalar.dma_start(
                out=out_2[:, 4 * q : 4 * q + 4, :].bitcast(I32).rearrange("g r c -> r g c"),
                in_=y_s[32 * q : 32 * q + 4, :, :].bitcast(I32),
            )
